import numpy as np
import ml_dtypes


def mxq(x, axis, fmt="e4m3"):
    dtype, down = {"e4m3": (ml_dtypes.float8_e4m3fn, 7), "e5m2": (ml_dtypes.float8_e5m2, 14)}[fmt]
    v = np.moveaxis(np.asarray(x, np.float32).astype(ml_dtypes.bfloat16).astype(np.float64), axis, -1)
    blocks = v.reshape(v.shape[:-1] + (-1, 32))
    amax = np.abs(blocks).max(-1, keepdims=True)
    byte = np.maximum(np.where(amax > 0, np.frexp(amax)[1] - 1 + 127, 0) - down, 1)
    scale = np.exp2(byte - 127.0)
    codes = (blocks / scale).astype(np.float32).astype(dtype).astype(np.float64)
    return np.moveaxis((codes * scale).reshape(v.shape), -1, axis)


WIDE = False


def mx_kscale(k):
    if not WIDE:
        return np.ones(k)
    levels = np.array([10, -10, 5, -5, 0])
    if k % 512:
        return np.exp2(np.random.permutation(np.resize(levels, k // 32))).repeat(32)
    a = np.empty((k // 512, 16))
    for p in range(k // 512):
        a[p, :8] = np.random.permutation(np.resize(levels, 8))
        for g in range(8):
            far = levels[np.abs(levels - a[p, g]) >= 10]
            a[p, g + 8] = far[np.random.randint(len(far))]
    return np.exp2(a.ravel()).repeat(32)


def f64(x):
    return np.asarray(x).astype(np.float64)


def striped(idx):
    return np.tile(np.asarray(idx).reshape(-1, 16).T, (8, 1)).astype(np.uint16)


def unstriped(offs):
    return offs[:16].T.reshape(-1).astype(np.int64)


E2M1 = np.array([0.0, 0.5, 1.0, 1.5, 2.0, 3.0, 4.0, 6.0, -0.0, -0.5, -1.0, -1.5, -2.0, -3.0, -4.0, -6.0])


def pack_weight(w, fmt):
    k, n = w.shape
    w = f64(np.asarray(w, np.float32).astype(ml_dtypes.bfloat16)).reshape(k // 32, 32, n)
    amax = np.abs(w).max(1)
    if fmt == "e4m3":
        byte = np.frexp(amax)[1] - 1 + 127 - 7
    else:
        mant, ex = np.frexp(amax / 6.0)
        byte = np.where(mant > 0.5, ex, ex - 1) + 127
    byte = np.clip(np.where(amax > 0, byte, 1), 1, 254)
    scaled = (w * np.exp2(127.0 - byte)[:, None, :]).reshape(k, n).astype(np.float32)
    by_word = np.ascontiguousarray(scaled.reshape(k // 512, 128, 4, n).transpose(0, 1, 3, 2))
    if fmt == "e4m3":
        words = by_word.astype(ml_dtypes.float8_e4m3fn).view(np.uint8)
    else:
        c = by_word.astype(ml_dtypes.float4_e2m1fn).view(np.uint8) & 0xF
        words = (c[..., 0::2] | (c[..., 1::2] << 4)).reshape(k // 512, 128, 2 * n)
    return np.ascontiguousarray(words), np.ascontiguousarray(byte.astype(np.uint8).reshape(k // 512, 16, n))


def unpack_weight(words, scales, fmt):
    g, _, n = scales.shape
    words = np.ascontiguousarray(words).reshape(g, 128, n, -1)
    if fmt == "e4m3":
        vals = words.view(ml_dtypes.float8_e4m3fn).astype(np.float64)
    else:
        nib = np.empty((g, 128, n, 4), np.uint8)
        nib[..., 0::2] = words & 0xF
        nib[..., 1::2] = words >> 4
        vals = E2M1[nib]
    vals = vals * np.repeat(np.exp2(scales.astype(np.float64) - 127.0), 8, axis=1)[..., None]
    return vals.transpose(0, 1, 3, 2).reshape(g * 512, n)


def bf(x):
    return np.asarray(x, np.float32).astype(ml_dtypes.bfloat16)


def planes(Y):
    r, m = Y.shape
    b = f64(bf(Y)).reshape(r // 32, 32, m)
    amax = np.abs(b).max(1)
    byte = np.clip(np.where(amax > 0, np.frexp(amax)[1] - 1 + 127 - 7, 1), 1, 254)
    codes = (b * np.exp2(127.0 - byte)[:, None, :]).reshape(r, m).astype(np.float32).astype(ml_dtypes.float8_e4m3fn).view(np.uint8)
    words = codes.reshape(r // 512, 128, 4, m).transpose(0, 1, 3, 2)
    return np.ascontiguousarray(words), np.ascontiguousarray(byte.astype(np.uint8).reshape(r // 512, 16, m))


K, T, J, N = 512, 512, 512, 512


def setup_inputs():
    n = np.random.standard_normal
    idx = np.random.randint(0, T, J)
    idx2 = np.random.randint(0, T, J)
    idx3 = np.random.randint(0, T, J)
    fk = mx_kscale(K)
    xtp = pack_weight(n((K, T)) / fk[:, None], "e2m1")
    wap = pack_weight(n((K, N)) * 1 / np.sqrt(K) * fk[:, None], "e4m3")
    wcp = pack_weight(n((K, N)) * 1 / np.sqrt(K) * fk[:, None], "e2m1")
    return {
        "xt_words": xtp[0],
        "xt_scales": xtp[1],
        "wa_words": wap[0],
        "wa_scales": wap[1],
        "wb": (n((K, N)) * 1 / np.sqrt(K) * fk[:, None]).astype(np.float32),
        "wc_words": wcp[0],
        "wc_scales": wcp[1],
        "offs": striped(idx),
        "offs2": striped(idx2),
        "offs3": striped(idx3),
    }


def reference(xt_words, xt_scales, wa_words, wa_scales, wb, wc_words, wc_scales, offs, offs2, offs3):
    idx = unstriped(offs)
    idx2 = unstriped(offs2)
    idx3 = unstriped(offs3)
    xtu = unpack_weight(xt_words, xt_scales, "e2m1")
    wau = unpack_weight(wa_words, wa_scales, "e4m3")
    wcu = unpack_weight(wc_words, wc_scales, "e2m1")
    za = wau.T @ xtu
    wbq = mxq(f64(wb), 0, "e4m3")
    zb = wbq.T @ xtu
    zc = wcu.T @ xtu
    lo = np.minimum(za[:, idx], zb[:, idx2])
    hi = np.maximum(za[:, idx], zb[:, idx2])
    y = np.maximum(lo, np.minimum(hi, zc[:, idx3]))
    words, scales = planes(y)
    return y, words, scales

@@ -1,0 +1,146 @@
+from contextlib import ExitStack
+
+import concourse.mybir as mybir
+
+K, T, J, N = 512, 512, 512, 512
+FLOPS = 3 * 2 * K * N * T
+
+F32 = mybir.dt.float32
+BF16 = mybir.dt.bfloat16
+I32 = mybir.dt.int32
+U16 = mybir.dt.uint16
+U8 = mybir.dt.uint8
+FP8X4 = mybir.dt.float8_e4m3fn_x4
+FP4X4 = mybir.dt.float4_e2m1fn_x4
+ALU = mybir.AluOpType
+
+P = 128
+PACK = 4
+HALF = 256
+PIECES = ((0, 256), (256, 128), (384, 128))
+
+
+def tile_list_middle_of_three_pl_kernel(
+    tc, xt_words, xt_scales, wa_words, wa_scales, wb, wc_words, wc_scales, offs, offs2, offs3, out_0, out_1, out_2
+):
+    nc = tc.nc
+    with ExitStack() as ctx:
+        keep = ctx.enter_context(tc.tile_pool(name="keep", bufs=1))
+        shared = ctx.enter_context(tc.tile_pool(name="shared", bufs=1))
+        psum = ctx.enter_context(tc.psum_pool(name="psum", bufs=8))
+
+        def load_scales(plane, rows, queue):
+            for q in range(4):
+                queue.dma_start(out=plane[32 * q : 32 * q + 4, :].bitcast(I32), in_=rows[0, 4 * q : 4 * q + 4, :].bitcast(I32))
+
+        wa_s_raw = keep.tile([P, N], U8, name="wa_s_raw", align_bytes=64)
+        xt_s = keep.tile([P, T], U8, name="xt_s", align_bytes=64)
+        wc_s_raw = keep.tile([P, N], U8, name="wc_s_raw", align_bytes=64)
+        for plane in (wa_s_raw, xt_s, wc_s_raw):
+            nc.vector.memset(plane[:].bitcast(I32), 0)
+
+        wa_raw = keep.tile([P, N], I32, name="wa_raw", align_bytes=64)
+        xt_w = keep.tile([P, 2 * T], U8, name="xt_w", align_bytes=64)
+        wc_raw = keep.tile([P, 2 * N], U8, name="wc_raw", align_bytes=64)
+        wb_raw = shared.tile([P, PACK, N], F32, name="wb_raw", offset=0)
+        list_a = keep.tile([P, J // 16], U16, name="list_a")
+        list_b = keep.tile([P, J // 16], U16, name="list_b")
+        list_c = keep.tile([P, J // 16], U16, name="list_c")
+
+        nc.sync.dma_start(out=wa_raw[:], in_=wa_words[0].rearrange("p n t -> p (n t)").bitcast(I32))
+        nc.sync.dma_start(out=xt_w[:].bitcast(I32), in_=xt_words[0].bitcast(I32))
+        load_scales(wa_s_raw, wa_scales, nc.sync)
+        load_scales(xt_s, xt_scales, nc.sync)
+        nc.sync.dma_start(list_a[:], offs)
+        nc.sync.dma_start(out=wc_raw[:].bitcast(I32), in_=wc_words[0].bitcast(I32))
+        load_scales(wc_s_raw, wc_scales, nc.sync)
+        nc.sync.dma_start(out=wb_raw[:], in_=wb.rearrange("(p j) n -> p j n", j=PACK))
+        nc.sync.dma_start(list_c[:], offs3)
+        nc.sync.dma_start(list_b[:], offs2)
+
+        def deal(dealt, raw):
+            nc.vector.tensor_copy(out=dealt.rearrange("p (t m) -> p m t", t=PACK), in_=raw.rearrange("p (m t) -> p m t", t=PACK))
+
+        def product(name, codes, scales, slices, place):
+            tables = []
+            for t in slices:
+                bank = psum.tile([P, T], F32, name="bank")
+                nc.tensor.matmul_mx(
+                    out=bank[:], lhsT=codes(t), lhsT_scale=scales[:, P * t : P * (t + 1)],
+                    rhs=xt_w[:].bitcast(FP4X4), rhs_scale=xt_s[:], start=True, stop=True,
+                )
+                table = place("%s%d" % (name, t), t)
+                nc.scalar.copy(out=table[:], in_=bank[:])
+                tables.append(table)
+            return tables
+
+        def own_bytes(name, t):
+            return keep.tile([P, T], F32, name=name)
+
+        def wb_raw_bytes(name, t):
+            return shared.tile([P, T], F32, name=name, offset=4 * T * t)
+
+        def looked_up(table, offsets, j0, width):
+            return table[:].indirect(offsets[:, j0 // 16 : (j0 + width) // 16])
+
+        def halves(name):
+            return [keep.tile([P, PACK, HALF], F32, name="%s%d" % (name, h)) for h in range(J // HALF)]
+
+        wa_w = keep.tile([P, N], I32, name="wa_w", align_bytes=64)
+        wa_s = keep.tile([P, N], U8, name="wa_s", align_bytes=64)
+        deal(wa_w[:], wa_raw[:])
+        deal(wa_s[:], wa_s_raw[:])
+        za = product("za", lambda t: wa_w[:, P * t : P * (t + 1)].bitcast(FP8X4), wa_s, range(PACK), own_bytes)
+
+        wc_w = keep.tile([P, 2 * N], U8, name="wc_w", align_bytes=64)
+        wc_s = keep.tile([P, N], U8, name="wc_s", align_bytes=64)
+        deal(wc_w[:].bitcast(U16), wc_raw[:].bitcast(U16))
+        deal(wc_s[:], wc_s_raw[:])
+        zc = product("zc", lambda t: wc_w[:, 2 * P * t : 2 * P * (t + 1)].bitcast(FP4X4), wc_s, range(1), own_bytes)
+
+        wb_bf = keep.tile([P, PACK * N], BF16, name="wb_bf", align_bytes=64)
+        wb_w = keep.tile([P, N], I32, name="wb_w", align_bytes=64)
+        wb_s = keep.tile([P, N], U8, name="wb_s", align_bytes=64)
+        nc.scalar.copy(
+            out=wb_bf[:].rearrange("p (t m j) -> p m j t", t=PACK, j=PACK),
+            in_=wb_raw[:].rearrange("p j (m t) -> p m j t", t=PACK),
+        )
+        nc.vector.quantize_mx(out=wb_w[:].bitcast(FP8X4), scales=wb_s[:], in_=wb_bf[:])
+        zc = zc + product("zc", lambda t: wc_w[:, 2 * P * t : 2 * P * (t + 1)].bitcast(FP4X4), wc_s, range(1, PACK), wb_raw_bytes)
+        zb = product("zb", lambda t: wb_w[:, P * t : P * (t + 1)].bitcast(FP8X4), wb_s, range(PACK), own_bytes)
+
+        a, db, dc = halves("a"), halves("db"), halves("dc")
+        for t in range(PACK):
+            for h in range(J // HALF):
+                nc.vector.tensor_copy(out=a[h][:, t, :], in_=looked_up(za[t], list_a, HALF * h, HALF))
+        for t in range(PACK):
+            for h in range(J // HALF):
+                nc.vector.tensor_tensor(out=dc[h][:, t, :], in0=looked_up(zc[t], list_c, HALF * h, HALF), in1=a[h][:, t, :], op=ALU.subtract)
+
+        y_w = keep.tile([P, J], I32, name="y_w", align_bytes=64)
+        y_s = keep.tile([P, J], U8, name="y_s", align_bytes=64)
+        y_rows = out_0.rearrange("(p t) j -> p t j", t=PACK)
+        y_words = out_1[0].rearrange("p n t -> p (n t)").bitcast(I32)
+        for i, (j0, width) in enumerate(PIECES):
+            h, c0 = divmod(j0, HALF)
+            cols = slice(c0, c0 + width)
+            for t in range(PACK):
+                nc.vector.tensor_tensor(out=db[h][:, t, cols], in0=looked_up(zb[t], list_b, j0, width), in1=a[h][:, t, cols], op=ALU.subtract)
+            capped = keep.tile([P, PACK, width], F32, name="capped%d" % i)
+            middle = keep.tile([P, PACK, width], F32, name="middle%d" % i)
+            y = keep.tile([P, PACK, width], F32, name="y%d" % i)
+            nc.vector.scalar_tensor_tensor(out=capped[:], in0=dc[h][:, :, cols], scalar=0.0, in1=db[h][:, :, cols], op0=ALU.max, op1=ALU.min)
+            nc.vector.scalar_tensor_tensor(out=middle[:], in0=dc[h][:, :, cols], scalar=0.0, in1=capped[:], op0=ALU.min, op1=ALU.max)
+            nc.vector.tensor_tensor(out=y[:], in0=middle[:], in1=a[h][:, :, cols], op=ALU.add)
+            nc.sync.dma_start(out=y_rows[:, :, j0 : j0 + width], in_=y[:])
+            y_bf = keep.tile([P, PACK * width], BF16, name="y_bf%d" % i, align_bytes=64)
+            cast = nc.vector.tensor_copy if i == len(PIECES) - 1 else nc.scalar.copy
+            cast(
+                out=y_bf[:].rearrange("p (c i t) -> p c t i", t=PACK, i=4),
+                in_=y[:].rearrange("p t (c i) -> p c t i", i=4),
+            )
+            nc.vector.quantize_mx(out=y_w[:, j0 : j0 + width].bitcast(FP8X4), scales=y_s[:, j0 : j0 + width], in_=y_bf[:])
+            nc.sync.dma_start(out=y_words[:, j0 : j0 + width], in_=y_w[:, j0 : j0 + width])
+        for q in range(4):
+            queue = nc.scalar if q % 2 else nc.sync
+            queue.dma_start(out=out_2[0, 4 * q : 4 * q + 4, :].bitcast(I32), in_=y_s[32 * q : 32 * q + 4, :].bitcast(I32))

@@ -1,6 +1,7 @@
 from contextlib import ExitStack
 
 import concourse.mybir as mybir
+from concourse.masks import make_identity
 
 K, T, J, N = 512, 512, 512, 512
 FLOPS = 3 * 2 * K * N * T
@@ -17,7 +18,6 @@ ALU = mybir.AluOpType
 P = 128
 PACK = 4
 HALF = 256
-PIECES = ((0, 256), (256, 128), (384, 128))
 
 
 def tile_list_middle_of_three_pl_kernel(
@@ -27,17 +27,22 @@ def tile_list_middle_of_three_pl_kernel(
     with ExitStack() as ctx:
         keep = ctx.enter_context(tc.tile_pool(name="keep", bufs=1))
         shared = ctx.enter_context(tc.tile_pool(name="shared", bufs=1))
-        psum = ctx.enter_context(tc.psum_pool(name="psum", bufs=8))
+        late = ctx.enter_context(tc.tile_pool(name="late", bufs=1))
+        psum = ctx.enter_context(tc.psum_pool(name="psum", bufs=4))
+        turns = ctx.enter_context(tc.psum_pool(name="turns", bufs=2))
+        stage = ctx.enter_context(tc.tile_pool(name="stage", bufs=2))
 
-        def load_scales(plane, rows, queue):
-            for q in range(4):
+        def load_scales(plane, rows, queue, quadrants):
+            for q in quadrants:
                 queue.dma_start(out=plane[32 * q : 32 * q + 4, :].bitcast(I32), in_=rows[0, 4 * q : 4 * q + 4, :].bitcast(I32))
 
         wa_s_raw = keep.tile([P, N], U8, name="wa_s_raw", align_bytes=64)
         xt_s = keep.tile([P, T], U8, name="xt_s", align_bytes=64)
         wc_s_raw = keep.tile([P, N], U8, name="wc_s_raw", align_bytes=64)
-        for plane in (wa_s_raw, xt_s, wc_s_raw):
+        for plane in (wa_s_raw, wc_s_raw):
             nc.vector.memset(plane[:].bitcast(I32), 0)
+        identity = keep.tile([P, P], F32, name="identity")
+        make_identity(nc, identity[:])
 
         wa_raw = keep.tile([P, N], I32, name="wa_raw", align_bytes=64)
         xt_w = keep.tile([P, 2 * T], U8, name="xt_w", align_bytes=64)
@@ -47,13 +52,14 @@ def tile_list_middle_of_three_pl_kernel(
         list_b = keep.tile([P, J // 16], U16, name="list_b")
         list_c = keep.tile([P, J // 16], U16, name="list_c")
 
+        load_scales(xt_s, xt_scales, nc.sync, (0, 1))
         nc.sync.dma_start(out=wa_raw[:], in_=wa_words[0].rearrange("p n t -> p (n t)").bitcast(I32))
+        load_scales(wa_s_raw, wa_scales, nc.sync, range(4))
         nc.sync.dma_start(out=xt_w[:].bitcast(I32), in_=xt_words[0].bitcast(I32))
-        load_scales(wa_s_raw, wa_scales, nc.sync)
-        load_scales(xt_s, xt_scales, nc.sync)
+        load_scales(xt_s, xt_scales, nc.sync, (2, 3))
         nc.sync.dma_start(list_a[:], offs)
         nc.sync.dma_start(out=wc_raw[:].bitcast(I32), in_=wc_words[0].bitcast(I32))
-        load_scales(wc_s_raw, wc_scales, nc.sync)
+        load_scales(wc_s_raw, wc_scales, nc.sync, range(4))
         nc.sync.dma_start(out=wb_raw[:], in_=wb.rearrange("(p j) n -> p j n", j=PACK))
         nc.sync.dma_start(list_c[:], offs3)
         nc.sync.dma_start(list_b[:], offs2)
@@ -96,7 +102,6 @@ def tile_list_middle_of_three_pl_kernel(
         wc_s = keep.tile([P, N], U8, name="wc_s", align_bytes=64)
         deal(wc_w[:].bitcast(U16), wc_raw[:].bitcast(U16))
         deal(wc_s[:], wc_s_raw[:])
-        zc = product("zc", lambda t: wc_w[:, 2 * P * t : 2 * P * (t + 1)].bitcast(FP4X4), wc_s, range(1), own_bytes)
 
         wb_bf = keep.tile([P, PACK * N], BF16, name="wb_bf", align_bytes=64)
         wb_w = keep.tile([P, N], I32, name="wb_w", align_bytes=64)
@@ -106,41 +111,78 @@ def tile_list_middle_of_three_pl_kernel(
             in_=wb_raw[:].rearrange("p j (m t) -> p m j t", t=PACK),
         )
         nc.vector.quantize_mx(out=wb_w[:].bitcast(FP8X4), scales=wb_s[:], in_=wb_bf[:])
-        zc = zc + product("zc", lambda t: wc_w[:, 2 * P * t : 2 * P * (t + 1)].bitcast(FP4X4), wc_s, range(1, PACK), wb_raw_bytes)
+        zc = product("zc", lambda t: wc_w[:, 2 * P * t : 2 * P * (t + 1)].bitcast(FP4X4), wc_s, range(PACK), wb_raw_bytes)
         zb = product("zb", lambda t: wb_w[:, P * t : P * (t + 1)].bitcast(FP8X4), wb_s, range(PACK), own_bytes)
 
-        a, db, dc = halves("a"), halves("db"), halves("dc")
+        a = halves("a")
         for t in range(PACK):
             for h in range(J // HALF):
                 nc.vector.tensor_copy(out=a[h][:, t, :], in_=looked_up(za[t], list_a, HALF * h, HALF))
-        for t in range(PACK):
-            for h in range(J // HALF):
-                nc.vector.tensor_tensor(out=dc[h][:, t, :], in0=looked_up(zc[t], list_c, HALF * h, HALF), in1=a[h][:, t, :], op=ALU.subtract)
 
         y_w = keep.tile([P, J], I32, name="y_w", align_bytes=64)
         y_s = keep.tile([P, J], U8, name="y_s", align_bytes=64)
         y_rows = out_0.rearrange("(p t) j -> p t j", t=PACK)
         y_words = out_1[0].rearrange("p n t -> p (n t)").bitcast(I32)
-        for i, (j0, width) in enumerate(PIECES):
-            h, c0 = divmod(j0, HALF)
-            cols = slice(c0, c0 + width)
+        blocks = [slice(b0, b0 + P) for b0 in range(0, HALF, P)]
+
+        def difference(name, slot, tables, offsets, h):
+            diff = late.tile([P, PACK, HALF], F32, name=name, offset=4096 * slot)
             for t in range(PACK):
-                nc.vector.tensor_tensor(out=db[h][:, t, cols], in0=looked_up(zb[t], list_b, j0, width), in1=a[h][:, t, cols], op=ALU.subtract)
-            capped = keep.tile([P, PACK, width], F32, name="capped%d" % i)
-            middle = keep.tile([P, PACK, width], F32, name="middle%d" % i)
-            y = keep.tile([P, PACK, width], F32, name="y%d" % i)
-            nc.vector.scalar_tensor_tensor(out=capped[:], in0=dc[h][:, :, cols], scalar=0.0, in1=db[h][:, :, cols], op0=ALU.max, op1=ALU.min)
-            nc.vector.scalar_tensor_tensor(out=middle[:], in0=dc[h][:, :, cols], scalar=0.0, in1=capped[:], op0=ALU.min, op1=ALU.max)
-            nc.vector.tensor_tensor(out=y[:], in0=middle[:], in1=a[h][:, :, cols], op=ALU.add)
-            nc.sync.dma_start(out=y_rows[:, :, j0 : j0 + width], in_=y[:])
-            y_bf = keep.tile([P, PACK * width], BF16, name="y_bf%d" % i, align_bytes=64)
-            cast = nc.vector.tensor_copy if i == len(PIECES) - 1 else nc.scalar.copy
+                nc.vector.tensor_tensor(out=diff[:, t, :], in0=looked_up(tables[t], offsets, HALF * h, HALF), in1=a[h][:, t, :], op=ALU.subtract)
+            return diff
+
+        def middle_difference(h, dc_slot, db_slot, capped_slot):
+            dc = difference("dc%d" % h, dc_slot, zc, list_c, h)
+            db = difference("db%d" % h, db_slot, zb, list_b, h)
+            capped = late.tile([P, PACK, HALF], F32, name="capped%d" % h, offset=4096 * capped_slot)
+            middle = [keep.tile([P, PACK, P], F32, name="middle%d_%d" % (h, i)) for i in range(len(blocks))]
+            for cols in blocks:
+                nc.vector.scalar_tensor_tensor(out=capped[:, :, cols], in0=dc[:, :, cols], scalar=0.0, in1=db[:, :, cols], op0=ALU.max, op1=ALU.min)
+            for i, cols in enumerate(blocks):
+                nc.vector.scalar_tensor_tensor(out=middle[i][:], in0=dc[:, :, cols], scalar=0.0, in1=capped[:, :, cols], op0=ALU.min, op1=ALU.max)
+            return middle
+
+        def quantize(y_bf, j0, width):
+            nc.vector.quantize_mx(out=y_w[:, j0 : j0 + width].bitcast(FP8X4), scales=y_s[:, j0 : j0 + width], in_=y_bf[:])
+
+        middle = middle_difference(0, 0, 1, 2)
+        y_bf = keep.tile([P, PACK * HALF], BF16, name="y_bf0", align_bytes=64)
+        for i, cols in enumerate(blocks):
+            turned = turns.tile([P, PACK, P], F32, name="turned")
+            for t in range(PACK):
+                nc.tensor.matmul(turned[:, t, :], a[0][:, t, cols], identity[:], start=True, stop=False, is_transpose=True)
+                nc.tensor.matmul(turned[:, t, :], middle[i][:, t, :], identity[:], start=False, stop=True, is_transpose=True)
+            turned_sb = stage.tile([P, PACK, P], F32, name="turned_sb")
+            nc.scalar.copy(out=turned_sb[:], in_=turned[:])
+            back = turns.tile([P, PACK, P], F32, name="back")
+            for t in range(PACK):
+                nc.tensor.transpose(back[:, t, :], turned_sb[:, t, :], identity[:])
+            y = keep.tile([P, PACK, P], F32, name="y0_%d" % i)
+            nc.scalar.copy(out=y[:], in_=back[:])
+            nc.sync.dma_start(out=y_rows[:, :, cols], in_=y[:])
+            nc.scalar.copy(
+                out=y_bf[:, PACK * cols.start : PACK * cols.stop].rearrange("p (c t) -> p c t", t=PACK),
+                in_=back[:].rearrange("p t c -> p c t"),
+            )
+        quantize(y_bf, 0, HALF)
+        nc.sync.dma_start(out=y_words[:, 0:HALF], in_=y_w[:, 0:HALF])
+
+        middle = middle_difference(1, 1, 2, 3)
+        ys = []
+        for i, cols in enumerate(blocks):
+            y = keep.tile([P, PACK, P], F32, name="y1_%d" % i)
+            nc.vector.tensor_tensor(out=y[:], in0=middle[i][:], in1=a[1][:, :, cols], op=ALU.add)
+            nc.sync.dma_start(out=y_rows[:, :, HALF + cols.start : HALF + cols.stop], in_=y[:])
+            ys.append(y)
+        for i, cols in enumerate(blocks):
+            y_bf = keep.tile([P, PACK * P], BF16, name="y_bf1_%d" % i, align_bytes=64)
+            cast = nc.vector.tensor_copy if i == len(blocks) - 1 else nc.scalar.copy
             cast(
                 out=y_bf[:].rearrange("p (c i t) -> p c t i", t=PACK, i=4),
-                in_=y[:].rearrange("p t (c i) -> p c t i", i=4),
+                in_=ys[i][:].rearrange("p t (c i) -> p c t i", i=4),
             )
-            nc.vector.quantize_mx(out=y_w[:, j0 : j0 + width].bitcast(FP8X4), scales=y_s[:, j0 : j0 + width], in_=y_bf[:])
-            nc.sync.dma_start(out=y_words[:, j0 : j0 + width], in_=y_w[:, j0 : j0 + width])
+            quantize(y_bf, HALF + cols.start, P)
+        nc.sync.dma_start(out=y_words[:, HALF:J], in_=y_w[:, HALF:J])
         for q in range(4):
             queue = nc.scalar if q % 2 else nc.sync
             queue.dma_start(out=out_2[0, 4 * q : 4 * q + 4, :].bitcast(I32), in_=y_s[32 * q : 32 * q + 4, :].bitcast(I32))

@@ -17,7 +17,11 @@ ALU = mybir.AluOpType
 
 P = 128
 PACK = 4
-HALF = 256
+BLOCKS = J // P
+FRONT = J // 2
+SPARE = 8
+SLOT = 4 * PACK * P
+ACT = mybir.ActivationFunctionType
 
 
 def tile_list_middle_of_three_pl_kernel(
@@ -28,9 +32,8 @@ def tile_list_middle_of_three_pl_kernel(
         keep = ctx.enter_context(tc.tile_pool(name="keep", bufs=1))
         shared = ctx.enter_context(tc.tile_pool(name="shared", bufs=1))
         late = ctx.enter_context(tc.tile_pool(name="late", bufs=1))
-        psum = ctx.enter_context(tc.psum_pool(name="psum", bufs=4))
-        turns = ctx.enter_context(tc.psum_pool(name="turns", bufs=2))
-        stage = ctx.enter_context(tc.tile_pool(name="stage", bufs=2))
+        psum = ctx.enter_context(tc.psum_pool(name="psum", bufs=5))
+        turns = ctx.enter_context(tc.psum_pool(name="turns", bufs=3))
 
         def load_scales(plane, rows, queue, quadrants):
             for q in quadrants:
@@ -41,6 +44,8 @@ def tile_list_middle_of_three_pl_kernel(
         wc_s_raw = keep.tile([P, N], U8, name="wc_s_raw", align_bytes=64)
         for plane in (wa_s_raw, wc_s_raw):
             nc.vector.memset(plane[:].bitcast(I32), 0)
+        minus_one = keep.tile([P, J], F32, name="minus_one")
+        nc.gpsimd.memset(minus_one[:], -1.0)
         identity = keep.tile([P, P], F32, name="identity")
         make_identity(nc, identity[:])
 
@@ -76,12 +81,17 @@ def tile_list_middle_of_three_pl_kernel(
                     rhs=xt_w[:].bitcast(FP4X4), rhs_scale=xt_s[:], start=True, stop=True,
                 )
                 table = place("%s%d" % (name, t), t)
-                nc.scalar.copy(out=table[:], in_=bank[:])
+                nc.scalar.copy(out=table[:, 0:T], in_=bank[:])
                 tables.append(table)
             return tables
 
         def own_bytes(name, t):
             return keep.tile([P, T], F32, name=name)
+
+        def with_spare(name, t):
+            table = keep.tile([P, T + SPARE], F32, name=name)
+            nc.gpsimd.memset(table[:, T : T + SPARE], 0.0)
+            return table
 
         def wb_raw_bytes(name, t):
             return shared.tile([P, T], F32, name=name, offset=4 * T * t)
@@ -89,14 +99,11 @@ def tile_list_middle_of_three_pl_kernel(
         def looked_up(table, offsets, j0, width):
             return table[:].indirect(offsets[:, j0 // 16 : (j0 + width) // 16])
 
-        def halves(name):
-            return [keep.tile([P, PACK, HALF], F32, name="%s%d" % (name, h)) for h in range(J // HALF)]
-
         wa_w = keep.tile([P, N], I32, name="wa_w", align_bytes=64)
         wa_s = keep.tile([P, N], U8, name="wa_s", align_bytes=64)
         deal(wa_w[:], wa_raw[:])
         deal(wa_s[:], wa_s_raw[:])
-        za = product("za", lambda t: wa_w[:, P * t : P * (t + 1)].bitcast(FP8X4), wa_s, range(PACK), own_bytes)
+        za = product("za", lambda t: wa_w[:, P * t : P * (t + 1)].bitcast(FP8X4), wa_s, range(PACK), with_spare)
 
         wc_w = keep.tile([P, 2 * N], U8, name="wc_w", align_bytes=64)
         wc_s = keep.tile([P, N], U8, name="wc_s", align_bytes=64)
@@ -104,7 +111,7 @@ def tile_list_middle_of_three_pl_kernel(
         deal(wc_s[:], wc_s_raw[:])
 
         wb_bf = keep.tile([P, PACK * N], BF16, name="wb_bf", align_bytes=64)
-        wb_w = keep.tile([P, N], I32, name="wb_w", align_bytes=64)
+        wb_w = late.tile([P, N], I32, name="wb_w", align_bytes=64, offset=3 * SLOT // 2)
         wb_s = keep.tile([P, N], U8, name="wb_s", align_bytes=64)
         nc.scalar.copy(
             out=wb_bf[:].rearrange("p (t m j) -> p m j t", t=PACK, j=PACK),
@@ -114,75 +121,102 @@ def tile_list_middle_of_three_pl_kernel(
         zc = product("zc", lambda t: wc_w[:, 2 * P * t : 2 * P * (t + 1)].bitcast(FP4X4), wc_s, range(PACK), wb_raw_bytes)
         zb = product("zb", lambda t: wb_w[:, P * t : P * (t + 1)].bitcast(FP8X4), wb_s, range(PACK), own_bytes)
 
-        a = halves("a")
+        neg_a = keep.tile([P, PACK, J], F32, name="neg_a")
         for t in range(PACK):
-            for h in range(J // HALF):
-                nc.vector.tensor_copy(out=a[h][:, t, :], in_=looked_up(za[t], list_a, HALF * h, HALF))
+            nc.vector.tensor_tensor(out=neg_a[:, t, :], in0=looked_up(za[t], list_a, 0, J), in1=minus_one[:], op=ALU.mult)
 
         y_w = keep.tile([P, J], I32, name="y_w", align_bytes=64)
         y_s = keep.tile([P, J], U8, name="y_s", align_bytes=64)
         y_rows = out_0.rearrange("(p t) j -> p t j", t=PACK)
         y_words = out_1[0].rearrange("p n t -> p (n t)").bitcast(I32)
-        blocks = [slice(b0, b0 + P) for b0 in range(0, HALF, P)]
+        front = [slice(b0, b0 + P) for b0 in range(0, FRONT, P)]
 
-        def difference(name, slot, tables, offsets, h):
-            diff = late.tile([P, PACK, HALF], F32, name=name, offset=4096 * slot)
+        def slot(name, index):
+            return late.tile([P, PACK, P], F32, name=name, align_bytes=64, offset=SLOT * index)
+
+        def difference(diff, tables, offsets, j0, width):
             for t in range(PACK):
-                nc.vector.tensor_tensor(out=diff[:, t, :], in0=looked_up(tables[t], offsets, HALF * h, HALF), in1=a[h][:, t, :], op=ALU.subtract)
-            return diff
+                nc.vector.tensor_tensor(out=diff[:, t, :], in0=looked_up(tables[t], offsets, j0, width), in1=neg_a[:, t, j0 : j0 + width], op=ALU.add)
 
-        def middle_difference(h, dc_slot, db_slot, capped_slot):
-            dc = difference("dc%d" % h, dc_slot, zc, list_c, h)
-            db = difference("db%d" % h, db_slot, zb, list_b, h)
-            capped = late.tile([P, PACK, HALF], F32, name="capped%d" % h, offset=4096 * capped_slot)
-            middle = [keep.tile([P, PACK, P], F32, name="middle%d_%d" % (h, i)) for i in range(len(blocks))]
-            for cols in blocks:
-                nc.vector.scalar_tensor_tensor(out=capped[:, :, cols], in0=dc[:, :, cols], scalar=0.0, in1=db[:, :, cols], op0=ALU.max, op1=ALU.min)
-            for i, cols in enumerate(blocks):
-                nc.vector.scalar_tensor_tensor(out=middle[i][:], in0=dc[:, :, cols], scalar=0.0, in1=capped[:, :, cols], op0=ALU.min, op1=ALU.max)
-            return middle
+        def turn(bank, rows, start, stop):
+            for t in range(PACK):
+                nc.tensor.matmul(
+                    bank[:, P * t : P * (t + 1)], rows[:, t, :], identity[:],
+                    start=start and t == 0, stop=stop and t == PACK - 1, is_transpose=True,
+                )
+
+        def by_slice(ap):
+            return ap.rearrange("p (t c) -> p t c", t=PACK)
 
         def quantize(y_bf, j0, width):
-            nc.vector.quantize_mx(out=y_w[:, j0 : j0 + width].bitcast(FP8X4), scales=y_s[:, j0 : j0 + width], in_=y_bf[:])
+            nc.vector.quantize_mx(out=y_w[:, j0 : j0 + width].bitcast(FP8X4), scales=y_s[:, j0 : j0 + width], in_=y_bf)
 
-        middle = middle_difference(0, 0, 1, 2)
-        y_bf = keep.tile([P, PACK * HALF], BF16, name="y_bf0", align_bytes=64)
-        for i, cols in enumerate(blocks):
-            turned = turns.tile([P, PACK, P], F32, name="turned")
-            for t in range(PACK):
-                nc.tensor.matmul(turned[:, t, :], a[0][:, t, cols], identity[:], start=True, stop=False, is_transpose=True)
-                nc.tensor.matmul(turned[:, t, :], middle[i][:, t, :], identity[:], start=False, stop=True, is_transpose=True)
-            turned_sb = stage.tile([P, PACK, P], F32, name="turned_sb")
-            nc.scalar.copy(out=turned_sb[:], in_=turned[:])
-            back = turns.tile([P, PACK, P], F32, name="back")
-            for t in range(PACK):
-                nc.tensor.transpose(back[:, t, :], turned_sb[:, t, :], identity[:])
-            y = keep.tile([P, PACK, P], F32, name="y0_%d" % i)
-            nc.scalar.copy(out=y[:], in_=back[:])
-            nc.sync.dma_start(out=y_rows[:, :, cols], in_=y[:])
+        dc = keep.tile([P, PACK, FRONT], F32, name="dc")
+        db = keep.tile([P, PACK, FRONT], F32, name="db")
+        difference(dc, zc, list_c, 0, FRONT)
+        difference(db, zb, list_b, 0, FRONT)
+
+        under = [slot("under%d" % i, 1 + i) for i in range(len(front))]
+        neg_lo_banks, above_banks, y_banks = [], [], []
+        for i, cols in enumerate(front):
+            nc.scalar.activation(out=under[i][:], in_=dc[:, :, cols], func=ACT.Relu, scale=-1.0)
+            neg_lo = turns.tile([P, PACK * P], F32, name="turned")
+            turn(neg_lo, neg_a[:, :, cols], True, False)
+            turn(neg_lo, under[i][:], False, True)
+            neg_lo_banks.append(neg_lo)
+            above = psum.tile([P, PACK * P], F32, name="bank")
+            turn(above, under[i][:], True, False)
+            above_banks.append(above)
+        for i, cols in enumerate(front):
+            lo_turned = keep.tile([P, PACK, P], F32, name="lo_turned%d" % i)
+            nc.scalar.activation(out=lo_turned[:], in_=by_slice(neg_lo_banks[i][:]), func=ACT.Copy, scale=-1.0)
+            y_bank = turns.tile([P, PACK * P], F32, name="turned")
+            turn(y_bank, lo_turned[:], True, False)
+            y_banks.append(y_bank)
+
+        y_bf = keep.tile([P, PACK * FRONT], BF16, name="y_bf", align_bytes=64)
+        for i, cols in enumerate(front):
+            capped = keep.tile([P, PACK, P], F32, name="capped%d" % i)
+            nc.vector.scalar_tensor_tensor(out=capped[:], in0=dc[:, :, cols], scalar=0.0, in1=db[:, :, cols], op0=ALU.max, op1=ALU.min)
+            turn(above_banks[i], capped[:], False, True)
+            above_turned = keep.tile([P, PACK, P], F32, name="above_turned%d" % i)
+            nc.scalar.activation(out=above_turned[:], in_=by_slice(above_banks[i][:]), func=ACT.Relu)
+            turn(y_banks[i], above_turned[:], False, True)
+            y = late.tile([P, PACK, P], F32, name="y%d" % i, align_bytes=64, offset=SLOT * (9 + 3 * i) // 2)
             nc.scalar.copy(
                 out=y_bf[:, PACK * cols.start : PACK * cols.stop].rearrange("p (c t) -> p c t", t=PACK),
-                in_=back[:].rearrange("p t c -> p c t"),
+                in_=y_banks[i][:].rearrange("p (t c) -> p c t", t=PACK),
             )
-        quantize(y_bf, 0, HALF)
-        nc.sync.dma_start(out=y_words[:, 0:HALF], in_=y_w[:, 0:HALF])
+            nc.scalar.copy(out=y[:], in_=by_slice(y_banks[i][:]))
+            nc.sync.dma_start(out=y_rows[:, :, cols], in_=y[:])
 
-        middle = middle_difference(1, 1, 2, 3)
-        ys = []
-        for i, cols in enumerate(blocks):
-            y = keep.tile([P, PACK, P], F32, name="y1_%d" % i)
-            nc.vector.tensor_tensor(out=y[:], in0=middle[i][:], in1=a[1][:, :, cols], op=ALU.add)
-            nc.sync.dma_start(out=y_rows[:, :, HALF + cols.start : HALF + cols.stop], in_=y[:])
-            ys.append(y)
-        for i, cols in enumerate(blocks):
-            y_bf = keep.tile([P, PACK * P], BF16, name="y_bf1_%d" % i, align_bytes=64)
-            cast = nc.vector.tensor_copy if i == len(blocks) - 1 else nc.scalar.copy
+        quantize(y_bf[:], 0, FRONT)
+        nc.sync.dma_start(out=y_words[:, 0:FRONT], in_=y_w[:, 0:FRONT])
+
+        dc_back = late.tile([P, PACK, J - FRONT], F32, name="dc_back", align_bytes=64, offset=0)
+        db_back = late.tile([P, PACK, J - FRONT], F32, name="db_back", align_bytes=64, offset=2 * SLOT)
+        difference(dc_back, zc, list_c, FRONT, J - FRONT)
+        difference(db_back, zb, list_b, FRONT, J - FRONT)
+        back = [slice(b0, b0 + P) for b0 in range(FRONT, J, P)]
+        capped = [keep.tile([P, PACK, P], F32, name="capped_back%d" % i) for i in range(len(back))]
+        middle = [keep.tile([P, PACK, P], F32, name="middle_back%d" % i) for i in range(len(back))]
+        ys = [slot("y_back%d" % i, 4 + i) for i in range(len(back))]
+        for i, cols in enumerate(back):
+            nc.vector.scalar_tensor_tensor(out=capped[i][:], in0=dc_back[:, :, P * i : P * (i + 1)], scalar=0.0, in1=db_back[:, :, P * i : P * (i + 1)], op0=ALU.max, op1=ALU.min)
+        for i, cols in enumerate(back):
+            nc.vector.scalar_tensor_tensor(out=middle[i][:], in0=dc_back[:, :, P * i : P * (i + 1)], scalar=0.0, in1=capped[i][:], op0=ALU.min, op1=ALU.max)
+        for i, cols in enumerate(back):
+            nc.vector.tensor_tensor(out=ys[i][:], in0=middle[i][:], in1=neg_a[:, :, cols], op=ALU.subtract)
+            nc.sync.dma_start(out=y_rows[:, :, cols], in_=ys[i][:])
+        for i, cols in enumerate(back):
+            y_bf_back = keep.tile([P, PACK * P], BF16, name="y_bf_back%d" % i, align_bytes=64)
+            cast = nc.vector.tensor_copy if i == len(back) - 1 else nc.scalar.copy
             cast(
-                out=y_bf[:].rearrange("p (c i t) -> p c t i", t=PACK, i=4),
+                out=y_bf_back[:].rearrange("p (c i t) -> p c t i", t=PACK, i=4),
                 in_=ys[i][:].rearrange("p t (c i) -> p c t i", i=4),
             )
-            quantize(y_bf, HALF + cols.start, P)
-        nc.sync.dma_start(out=y_words[:, HALF:J], in_=y_w[:, HALF:J])
+            quantize(y_bf_back[:], cols.start, P)
+        nc.sync.dma_start(out=y_words[:, FRONT:J], in_=y_w[:, FRONT:J])
         for q in range(4):
             queue = nc.scalar if q % 2 else nc.sync
             queue.dma_start(out=out_2[0, 4 * q : 4 * q + 4, :].bitcast(I32), in_=y_s[32 * q : 32 * q + 4, :].bitcast(I32))

from contextlib import ExitStack

import concourse.mybir as mybir
from concourse.masks import make_identity

K, T, J, N = 512, 512, 512, 512
FLOPS = 3 * 2 * K * N * T

F32 = mybir.dt.float32
BF16 = mybir.dt.bfloat16
I32 = mybir.dt.int32
U16 = mybir.dt.uint16
U8 = mybir.dt.uint8
FP8X4 = mybir.dt.float8_e4m3fn_x4
FP4X4 = mybir.dt.float4_e2m1fn_x4
ALU = mybir.AluOpType

P = 128
PACK = 4
BLOCKS = J // P
FRONT = J // 2
SPARE = 8
SLOT = 4 * PACK * P
ACT = mybir.ActivationFunctionType


def tile_list_middle_of_three_pl_kernel(
    tc, xt_words, xt_scales, wa_words, wa_scales, wb, wc_words, wc_scales, offs, offs2, offs3, out_0, out_1, out_2
):
    nc = tc.nc
    with ExitStack() as ctx:
        keep = ctx.enter_context(tc.tile_pool(name="keep", bufs=1))
        shared = ctx.enter_context(tc.tile_pool(name="shared", bufs=1))
        late = ctx.enter_context(tc.tile_pool(name="late", bufs=1))
        psum = ctx.enter_context(tc.psum_pool(name="psum", bufs=5))
        turns = ctx.enter_context(tc.psum_pool(name="turns", bufs=3))

        def load_scales(plane, rows, queue, quadrants):
            for q in quadrants:
                queue.dma_start(out=plane[32 * q : 32 * q + 4, :].bitcast(I32), in_=rows[0, 4 * q : 4 * q + 4, :].bitcast(I32))

        wa_s_raw = keep.tile([P, N], U8, name="wa_s_raw", align_bytes=64)
        xt_s = keep.tile([P, T], U8, name="xt_s", align_bytes=64)
        wc_s_raw = keep.tile([P, N], U8, name="wc_s_raw", align_bytes=64)
        for plane in (wa_s_raw, wc_s_raw):
            nc.vector.memset(plane[:].bitcast(I32), 0)
        minus_one = keep.tile([P, J], F32, name="minus_one")
        nc.gpsimd.memset(minus_one[:], -1.0)
        identity = keep.tile([P, P], F32, name="identity")
        make_identity(nc, identity[:])

        wa_raw = keep.tile([P, N], I32, name="wa_raw", align_bytes=64)
        xt_w = keep.tile([P, 2 * T], U8, name="xt_w", align_bytes=64)
        wc_raw = keep.tile([P, 2 * N], U8, name="wc_raw", align_bytes=64)
        wb_raw = shared.tile([P, PACK, N], F32, name="wb_raw", offset=0)
        list_a = keep.tile([P, J // 16], U16, name="list_a")
        list_b = keep.tile([P, J // 16], U16, name="list_b")
        list_c = keep.tile([P, J // 16], U16, name="list_c")

        load_scales(xt_s, xt_scales, nc.sync, (0, 1))
        nc.sync.dma_start(out=wa_raw[:], in_=wa_words[0].rearrange("p n t -> p (n t)").bitcast(I32))
        load_scales(wa_s_raw, wa_scales, nc.sync, range(4))
        nc.sync.dma_start(out=xt_w[:].bitcast(I32), in_=xt_words[0].bitcast(I32))
        load_scales(xt_s, xt_scales, nc.sync, (2, 3))
        nc.sync.dma_start(list_a[:], offs)
        nc.sync.dma_start(out=wc_raw[:].bitcast(I32), in_=wc_words[0].bitcast(I32))
        load_scales(wc_s_raw, wc_scales, nc.sync, range(4))
        nc.sync.dma_start(out=wb_raw[:], in_=wb.rearrange("(p j) n -> p j n", j=PACK))
        nc.sync.dma_start(list_c[:], offs3)
        nc.sync.dma_start(list_b[:], offs2)

        def deal(dealt, raw):
            nc.vector.tensor_copy(out=dealt.rearrange("p (t m) -> p m t", t=PACK), in_=raw.rearrange("p (m t) -> p m t", t=PACK))

        def product(name, codes, scales, slices, place):
            tables = []
            for t in slices:
                bank = psum.tile([P, T], F32, name="bank")
                nc.tensor.matmul_mx(
                    out=bank[:], lhsT=codes(t), lhsT_scale=scales[:, P * t : P * (t + 1)],
                    rhs=xt_w[:].bitcast(FP4X4), rhs_scale=xt_s[:], start=True, stop=True,
                )
                table = place("%s%d" % (name, t), t)
                nc.scalar.copy(out=table[:, 0:T], in_=bank[:])
                tables.append(table)
            return tables

        def own_bytes(name, t):
            return keep.tile([P, T], F32, name=name)

        def with_spare(name, t):
            table = keep.tile([P, T + SPARE], F32, name=name)
            nc.gpsimd.memset(table[:, T : T + SPARE], 0.0)
            return table

        def wb_raw_bytes(name, t):
            return shared.tile([P, T], F32, name=name, offset=4 * T * t)

        def looked_up(table, offsets, j0, width):
            return table[:].indirect(offsets[:, j0 // 16 : (j0 + width) // 16])

        wa_w = keep.tile([P, N], I32, name="wa_w", align_bytes=64)
        wa_s = keep.tile([P, N], U8, name="wa_s", align_bytes=64)
        deal(wa_w[:], wa_raw[:])
        deal(wa_s[:], wa_s_raw[:])
        za = product("za", lambda t: wa_w[:, P * t : P * (t + 1)].bitcast(FP8X4), wa_s, range(PACK), with_spare)

        wc_w = keep.tile([P, 2 * N], U8, name="wc_w", align_bytes=64)
        wc_s = keep.tile([P, N], U8, name="wc_s", align_bytes=64)
        deal(wc_w[:].bitcast(U16), wc_raw[:].bitcast(U16))
        deal(wc_s[:], wc_s_raw[:])

        wb_bf = keep.tile([P, PACK * N], BF16, name="wb_bf", align_bytes=64)
        wb_w = late.tile([P, N], I32, name="wb_w", align_bytes=64, offset=3 * SLOT // 2)
        wb_s = keep.tile([P, N], U8, name="wb_s", align_bytes=64)
        nc.scalar.copy(
            out=wb_bf[:].rearrange("p (t m j) -> p m j t", t=PACK, j=PACK),
            in_=wb_raw[:].rearrange("p j (m t) -> p m j t", t=PACK),
        )
        nc.vector.quantize_mx(out=wb_w[:].bitcast(FP8X4), scales=wb_s[:], in_=wb_bf[:])
        zc = product("zc", lambda t: wc_w[:, 2 * P * t : 2 * P * (t + 1)].bitcast(FP4X4), wc_s, range(PACK), wb_raw_bytes)
        zb = product("zb", lambda t: wb_w[:, P * t : P * (t + 1)].bitcast(FP8X4), wb_s, range(PACK), own_bytes)

        neg_a = keep.tile([P, PACK, J], F32, name="neg_a")
        for t in range(PACK):
            nc.vector.tensor_tensor(out=neg_a[:, t, :], in0=looked_up(za[t], list_a, 0, J), in1=minus_one[:], op=ALU.mult)

        y_w = keep.tile([P, J], I32, name="y_w", align_bytes=64)
        y_s = keep.tile([P, J], U8, name="y_s", align_bytes=64)
        y_rows = out_0.rearrange("(p t) j -> p t j", t=PACK)
        y_words = out_1[0].rearrange("p n t -> p (n t)").bitcast(I32)
        front = [slice(b0, b0 + P) for b0 in range(0, FRONT, P)]

        def slot(name, index):
            return late.tile([P, PACK, P], F32, name=name, align_bytes=64, offset=SLOT * index)

        def difference(diff, tables, offsets, j0, width):
            for t in range(PACK):
                nc.vector.tensor_tensor(out=diff[:, t, :], in0=looked_up(tables[t], offsets, j0, width), in1=neg_a[:, t, j0 : j0 + width], op=ALU.add)

        def turn(bank, rows, start, stop):
            for t in range(PACK):
                nc.tensor.matmul(
                    bank[:, P * t : P * (t + 1)], rows[:, t, :], identity[:],
                    start=start and t == 0, stop=stop and t == PACK - 1, is_transpose=True,
                )

        def by_slice(ap):
            return ap.rearrange("p (t c) -> p t c", t=PACK)

        def quantize(y_bf, j0, width):
            nc.vector.quantize_mx(out=y_w[:, j0 : j0 + width].bitcast(FP8X4), scales=y_s[:, j0 : j0 + width], in_=y_bf)

        dc = keep.tile([P, PACK, FRONT], F32, name="dc")
        db = keep.tile([P, PACK, FRONT], F32, name="db")
        difference(dc, zc, list_c, 0, FRONT)
        difference(db, zb, list_b, 0, FRONT)

        under = [slot("under%d" % i, 1 + i) for i in range(len(front))]
        neg_lo_banks, above_banks, y_banks = [], [], []
        for i, cols in enumerate(front):
            nc.scalar.activation(out=under[i][:], in_=dc[:, :, cols], func=ACT.Relu, scale=-1.0)
            neg_lo = turns.tile([P, PACK * P], F32, name="turned")
            turn(neg_lo, neg_a[:, :, cols], True, False)
            turn(neg_lo, under[i][:], False, True)
            neg_lo_banks.append(neg_lo)
            above = psum.tile([P, PACK * P], F32, name="bank")
            turn(above, under[i][:], True, False)
            above_banks.append(above)
        for i, cols in enumerate(front):
            lo_turned = keep.tile([P, PACK, P], F32, name="lo_turned%d" % i)
            nc.scalar.activation(out=lo_turned[:], in_=by_slice(neg_lo_banks[i][:]), func=ACT.Copy, scale=-1.0)
            y_bank = turns.tile([P, PACK * P], F32, name="turned")
            turn(y_bank, lo_turned[:], True, False)
            y_banks.append(y_bank)

        y_bf = keep.tile([P, PACK * FRONT], BF16, name="y_bf", align_bytes=64)
        for i, cols in enumerate(front):
            capped = keep.tile([P, PACK, P], F32, name="capped%d" % i)
            nc.vector.scalar_tensor_tensor(out=capped[:], in0=dc[:, :, cols], scalar=0.0, in1=db[:, :, cols], op0=ALU.max, op1=ALU.min)
            turn(above_banks[i], capped[:], False, True)
            above_turned = keep.tile([P, PACK, P], F32, name="above_turned%d" % i)
            nc.scalar.activation(out=above_turned[:], in_=by_slice(above_banks[i][:]), func=ACT.Relu)
            turn(y_banks[i], above_turned[:], False, True)
            y = late.tile([P, PACK, P], F32, name="y%d" % i, align_bytes=64, offset=SLOT * (9 + 3 * i) // 2)
            nc.scalar.copy(
                out=y_bf[:, PACK * cols.start : PACK * cols.stop].rearrange("p (c t) -> p c t", t=PACK),
                in_=y_banks[i][:].rearrange("p (t c) -> p c t", t=PACK),
            )
            nc.scalar.copy(out=y[:], in_=by_slice(y_banks[i][:]))
            nc.sync.dma_start(out=y_rows[:, :, cols], in_=y[:])

        quantize(y_bf[:], 0, FRONT)
        nc.sync.dma_start(out=y_words[:, 0:FRONT], in_=y_w[:, 0:FRONT])

        dc_back = late.tile([P, PACK, J - FRONT], F32, name="dc_back", align_bytes=64, offset=0)
        db_back = late.tile([P, PACK, J - FRONT], F32, name="db_back", align_bytes=64, offset=2 * SLOT)
        difference(dc_back, zc, list_c, FRONT, J - FRONT)
        difference(db_back, zb, list_b, FRONT, J - FRONT)
        back = [slice(b0, b0 + P) for b0 in range(FRONT, J, P)]
        capped = [keep.tile([P, PACK, P], F32, name="capped_back%d" % i) for i in range(len(back))]
        middle = [keep.tile([P, PACK, P], F32, name="middle_back%d" % i) for i in range(len(back))]
        ys = [slot("y_back%d" % i, 4 + i) for i in range(len(back))]
        for i, cols in enumerate(back):
            nc.vector.scalar_tensor_tensor(out=capped[i][:], in0=dc_back[:, :, P * i : P * (i + 1)], scalar=0.0, in1=db_back[:, :, P * i : P * (i + 1)], op0=ALU.max, op1=ALU.min)
        for i, cols in enumerate(back):
            nc.vector.scalar_tensor_tensor(out=middle[i][:], in0=dc_back[:, :, P * i : P * (i + 1)], scalar=0.0, in1=capped[i][:], op0=ALU.min, op1=ALU.max)
        for i, cols in enumerate(back):
            nc.vector.tensor_tensor(out=ys[i][:], in0=middle[i][:], in1=neg_a[:, :, cols], op=ALU.subtract)
            nc.sync.dma_start(out=y_rows[:, :, cols], in_=ys[i][:])
        for i, cols in enumerate(back):
            y_bf_back = keep.tile([P, PACK * P], BF16, name="y_bf_back%d" % i, align_bytes=64)
            cast = nc.vector.tensor_copy if i == len(back) - 1 else nc.scalar.copy
            cast(
                out=y_bf_back[:].rearrange("p (c i t) -> p c t i", t=PACK, i=4),
                in_=ys[i][:].rearrange("p t (c i) -> p c t i", i=4),
            )
            quantize(y_bf_back[:], cols.start, P)
        nc.sync.dma_start(out=y_words[:, FRONT:J], in_=y_w[:, FRONT:J])
        for q in range(4):
            queue = nc.scalar if q % 2 else nc.sync
            queue.dma_start(out=out_2[0, 4 * q : 4 * q + 4, :].bitcast(I32), in_=y_s[32 * q : 32 * q + 4, :].bitcast(I32))
